import numpy as np
import ml_dtypes

BF16 = ml_dtypes.bfloat16


def bf(x):
    return np.asarray(x, np.float32).astype(BF16)


def f32(x):
    return np.asarray(x, np.float32)


def f64(x):
    return np.asarray(x).astype(np.float64)


def striped(idx):
    return np.concatenate([l.reshape(-1, 16).T for l in idx])


def rows(idx, k):
    return np.tile(np.repeat(idx, 16, axis=0), (k // (16 * 8), 1))


def look(tab, idx):
    return np.take_along_axis(f64(tab), rows(idx, len(tab)), axis=1)


K, S, V, N, M = 512, 2048, 1024, 1024, 512


def angles():
    a = np.random.uniform(0.0, 2.0 * np.pi, (K, S))
    return np.stack([np.cos(a), np.sin(a)])


def setup_inputs():
    return {"tab": f32(angles()), "x0": f32(np.random.standard_normal((K, V))), "x1": f32(np.random.standard_normal((K, V))), "w": bf(np.random.standard_normal((K, M)) / np.sqrt(K)), "offs": striped(np.random.randint(0, S, (8, N)))}


def reference(tab, x0, x1, w, offs):
    idx = np.stack([g.T.reshape(-1) for g in np.split(offs, 8)])
    x = f64(x0) * look(tab[0], idx) + f64(x1) * look(tab[1], idx)
    y = f64(w).T @ x
    return y

@@ -1,0 +1,59 @@
+import concourse.mybir as mybir
+
+F32, BF16, U16 = mybir.dt.float32, mybir.dt.bfloat16, mybir.dt.uint16
+MULT, ADD = mybir.AluOpType.mult, mybir.AluOpType.add
+
+P = 128
+BANK = 512
+GROUP = 16
+
+FLOPS = 2 * 512 * 512 * 1024
+
+
+def tile_lookup_rope_mul_none_kernel(tc, tab, x0, x1, w, offs, out):
+    nc = tc.nc
+    rows, positions = tab.shape[1], tab.shape[2]
+    entries, features = x0.shape[1], w.shape[1]
+    row_blocks, out_blocks, halves = rows // P, features // P, entries // BANK
+
+    with (
+        tc.tile_pool(name="held", bufs=1) as held,
+        tc.psum_pool(name="psum", bufs=1) as psum,
+    ):
+        offsets = held.tile([P, entries // GROUP], U16, name="offsets")
+        nc.sync.dma_start(offsets[:], offs)
+        weights = held.tile([P, row_blocks, features], BF16, name="weights")
+        nc.sync.dma_start(weights[:], w.rearrange("(k p) m -> p k m", p=P))
+
+        banks = [[psum.tile([P, BANK], F32, name=f"bank{m}_{h}") for h in range(halves)]
+                 for m in range(out_blocks)]
+
+        for k in range(row_blocks):
+            block = slice(k * P, (k + 1) * P)
+            cosines = held.tile([P, positions], F32, name=f"cosines{k}")
+            values = held.tile([P, entries], F32, name=f"values{k}")
+            sines = held.tile([P, positions], F32, name=f"sines{k}")
+            turned = held.tile([P, entries], F32, name=f"turned{k}")
+            nc.sync.dma_start(cosines[:], tab[0, block, :])
+            nc.sync.dma_start(values[:], x0[block, :])
+            nc.sync.dma_start(sines[:], tab[1, block, :])
+            nc.sync.dma_start(turned[:], x1[block, :])
+
+            for h in range(halves):
+                cols = slice(h * BANK, (h + 1) * BANK)
+                piece = offsets[:, h * BANK // GROUP:(h + 1) * BANK // GROUP]
+                by_cos = held.tile([P, BANK], F32, name=f"by_cos{k}_{h}")
+                by_sin = held.tile([P, BANK], F32, name=f"by_sin{k}_{h}")
+                rotated = held.tile([P, BANK], BF16, name=f"rotated{k}_{h}")
+                nc.vector.tensor_tensor(by_cos[:], cosines[:].indirect(piece), values[:, cols], MULT)
+                nc.vector.tensor_tensor(by_sin[:], sines[:].indirect(piece), turned[:, cols], MULT)
+                nc.vector.tensor_tensor(rotated[:], by_cos[:], by_sin[:], ADD)
+                for m in range(out_blocks):
+                    nc.tensor.matmul(banks[m][h][:], weights[:, k, m * P:(m + 1) * P], rotated[:],
+                                     start=(k == 0), stop=(k == row_blocks - 1))
+
+        for h in range(halves):
+            for m in range(out_blocks):
+                staged = held.tile([P, BANK], F32, name=f"staged{m}_{h}")
+                nc.scalar.copy(staged[:], banks[m][h][:])
+                nc.sync.dma_start(out[m * P:(m + 1) * P, h * BANK:(h + 1) * BANK], staged[:])

@@ -6,6 +6,8 @@ MULT, ADD = mybir.AluOpType.mult, mybir.AluOpType.add
 P = 128
 BANK = 512
 GROUP = 16
+PIECE = 256
+EARLY = 2
 
 FLOPS = 2 * 512 * 512 * 1024
 
@@ -14,46 +16,80 @@ def tile_lookup_rope_mul_none_kernel(tc, tab, x0, x1, w, offs, out):
     nc = tc.nc
     rows, positions = tab.shape[1], tab.shape[2]
     entries, features = x0.shape[1], w.shape[1]
-    row_blocks, out_blocks, halves = rows // P, features // P, entries // BANK
+    row_blocks, out_blocks, pieces = rows // P, features // P, entries // PIECE
+    per_bank = BANK // PIECE
+    last = row_blocks - 1
+    out_rows = out.rearrange("(m p) j -> p m j", p=P)
 
     with (
         tc.tile_pool(name="held", bufs=1) as held,
         tc.psum_pool(name="psum", bufs=1) as psum,
     ):
+        def load(name, source):
+            tile = held.tile([P, source.shape[1]], F32, name=name)
+            nc.sync.dma_start(tile[:], source)
+            return tile
+
+        def looked_up_product(name, window, factor, first, count):
+            product = held.tile([P, count], F32, name=name)
+            entries_used = offsets[:, first // GROUP:(first + count) // GROUP]
+            nc.vector.tensor_tensor(product[:], window[:].indirect(entries_used), factor, MULT)
+            return product
+
+        def rounded_sum(name, by_cos, by_sin):
+            rotated = held.tile([P, by_cos.shape[1]], BF16, name=name)
+            nc.vector.tensor_tensor(rotated[:], by_cos, by_sin, ADD)
+            return rotated
+
+        def accumulate(k, q, rotated):
+            for m in range(out_blocks):
+                b, i = divmod(m, per_bank)
+                nc.tensor.matmul(banks[q][b][:, i, :], weights[:, k, m * P:(m + 1) * P], rotated,
+                                 start=(k == 0 and i == 0), stop=(k == last and i == per_bank - 1))
+
         offsets = held.tile([P, entries // GROUP], U16, name="offsets")
         nc.sync.dma_start(offsets[:], offs)
         weights = held.tile([P, row_blocks, features], BF16, name="weights")
-        nc.sync.dma_start(weights[:], w.rearrange("(k p) m -> p k m", p=P))
+        banks = [[psum.tile([P, per_bank, PIECE], F32, name=f"bank{q}_{b}")
+                  for b in range(out_blocks // per_bank)] for q in range(pieces)]
 
-        banks = [[psum.tile([P, BANK], F32, name=f"bank{m}_{h}") for h in range(halves)]
-                 for m in range(out_blocks)]
-
-        for k in range(row_blocks):
+        for k in range(last):
             block = slice(k * P, (k + 1) * P)
-            cosines = held.tile([P, positions], F32, name=f"cosines{k}")
-            values = held.tile([P, entries], F32, name=f"values{k}")
-            sines = held.tile([P, positions], F32, name=f"sines{k}")
-            turned = held.tile([P, entries], F32, name=f"turned{k}")
-            nc.sync.dma_start(cosines[:], tab[0, block, :])
-            nc.sync.dma_start(values[:], x0[block, :])
-            nc.sync.dma_start(sines[:], tab[1, block, :])
-            nc.sync.dma_start(turned[:], x1[block, :])
+            cosines = load(f"cosines{k}", tab[0, block, :])
+            values = load(f"values{k}", x0[block, :])
+            sines = load(f"sines{k}", tab[1, block, :])
+            turned = load(f"turned{k}", x1[block, :])
+            if k == 0:
+                nc.sync.dma_start(weights[:], w.rearrange("(k p) m -> p k m", p=P))
+            by_cos = looked_up_product(f"by_cos{k}", cosines, values[:], 0, entries)
+            by_sin = looked_up_product(f"by_sin{k}", sines, turned[:], 0, entries)
+            rotated = rounded_sum(f"rotated{k}", by_cos[:], by_sin[:])
+            for q in range(pieces):
+                accumulate(k, q, rotated[:, q * PIECE:(q + 1) * PIECE])
 
-            for h in range(halves):
-                cols = slice(h * BANK, (h + 1) * BANK)
-                piece = offsets[:, h * BANK // GROUP:(h + 1) * BANK // GROUP]
-                by_cos = held.tile([P, BANK], F32, name=f"by_cos{k}_{h}")
-                by_sin = held.tile([P, BANK], F32, name=f"by_sin{k}_{h}")
-                rotated = held.tile([P, BANK], BF16, name=f"rotated{k}_{h}")
-                nc.vector.tensor_tensor(by_cos[:], cosines[:].indirect(piece), values[:, cols], MULT)
-                nc.vector.tensor_tensor(by_sin[:], sines[:].indirect(piece), turned[:, cols], MULT)
-                nc.vector.tensor_tensor(rotated[:], by_cos[:], by_sin[:], ADD)
-                for m in range(out_blocks):
-                    nc.tensor.matmul(banks[m][h][:], weights[:, k, m * P:(m + 1) * P], rotated[:],
-                                     start=(k == 0), stop=(k == row_blocks - 1))
+        block = slice(last * P, rows)
+        cols = [slice(q * PIECE, (q + 1) * PIECE) for q in range(pieces)]
+        cosines = load("cosines_last", tab[0, block, :])
+        values = [load(f"values_last{q}", x0[block, cols[q]]) for q in range(EARLY)]
+        turned = [load("turned_last0", x1[block, cols[0]])]
+        sines = load("sines_last", tab[1, block, :])
+        for q in range(1, pieces):
+            if q >= EARLY:
+                values.append(load(f"values_last{q}", x0[block, cols[q]]))
+            turned.append(load(f"turned_last{q}", x1[block, cols[q]]))
 
-        for h in range(halves):
-            for m in range(out_blocks):
-                staged = held.tile([P, BANK], F32, name=f"staged{m}_{h}")
-                nc.scalar.copy(staged[:], banks[m][h][:])
-                nc.sync.dma_start(out[m * P:(m + 1) * P, h * BANK:(h + 1) * BANK], staged[:])
+        by_cos = [looked_up_product(f"by_cos_last{q}", cosines, values[q][:], q * PIECE, PIECE)
+                  for q in range(EARLY)]
+        for q in range(pieces):
+            if q >= EARLY:
+                by_cos.append(looked_up_product(f"by_cos_last{q}", cosines, values[q][:], q * PIECE, PIECE))
+            by_sin = looked_up_product(f"by_sin_last{q}", sines, turned[q][:], q * PIECE, PIECE)
+            rotated = rounded_sum(f"rotated_last{q}", by_cos[q][:], by_sin[:])
+            accumulate(last, q, rotated[:])
+            for b, bank in enumerate(banks[q]):
+                staged = held.tile([P, per_bank, PIECE], F32, name=f"staged{q}_{b}")
+                if q == pieces - 1 and b == len(banks[q]) - 1:
+                    nc.vector.tensor_copy(staged[:], bank[:])
+                else:
+                    nc.scalar.copy(staged[:], bank[:])
+                nc.sync.dma_start(out_rows[:, b * per_bank:(b + 1) * per_bank, cols[q]], staged[:])

@@ -7,6 +7,7 @@ P = 128
 BANK = 512
 GROUP = 16
 PIECE = 256
+STEP = 128
 EARLY = 2
 
 FLOPS = 2 * 512 * 512 * 1024
@@ -19,6 +20,7 @@ def tile_lookup_rope_mul_none_kernel(tc, tab, x0, x1, w, offs, out):
     row_blocks, out_blocks, pieces = rows // P, features // P, entries // PIECE
     per_bank = BANK // PIECE
     last = row_blocks - 1
+    w_rows = w.rearrange("(k p) m -> p k m", p=P)
     out_rows = out.rearrange("(m p) j -> p m j", p=P)
 
     with (
@@ -41,11 +43,11 @@ def tile_lookup_rope_mul_none_kernel(tc, tab, x0, x1, w, offs, out):
             nc.vector.tensor_tensor(rotated[:], by_cos, by_sin, ADD)
             return rotated
 
-        def accumulate(k, q, rotated):
+        def accumulate(k, q, rotated, inside, closes):
             for m in range(out_blocks):
                 b, i = divmod(m, per_bank)
-                nc.tensor.matmul(banks[q][b][:, i, :], weights[:, k, m * P:(m + 1) * P], rotated,
-                                 start=(k == 0 and i == 0), stop=(k == last and i == per_bank - 1))
+                nc.tensor.matmul(banks[q][b][:, i, inside], weights[:, k, m * P:(m + 1) * P], rotated,
+                                 start=(k == 0 and i == 0), stop=(closes and i == per_bank - 1))
 
         offsets = held.tile([P, entries // GROUP], U16, name="offsets")
         nc.sync.dma_start(offsets[:], offs)
@@ -53,26 +55,30 @@ def tile_lookup_rope_mul_none_kernel(tc, tab, x0, x1, w, offs, out):
         banks = [[psum.tile([P, per_bank, PIECE], F32, name=f"bank{q}_{b}")
                   for b in range(out_blocks // per_bank)] for q in range(pieces)]
 
+        cols = [slice(q * PIECE, (q + 1) * PIECE) for q in range(pieces)]
+        rotated = []
         for k in range(last):
             block = slice(k * P, (k + 1) * P)
             cosines = load(f"cosines{k}", tab[0, block, :])
             values = load(f"values{k}", x0[block, :])
+            if k == last - 1:
+                nc.sync.dma_start(weights[:, :last, :], w_rows[:, :last, :])
             sines = load(f"sines{k}", tab[1, block, :])
             turned = load(f"turned{k}", x1[block, :])
-            if k == 0:
-                nc.sync.dma_start(weights[:], w.rearrange("(k p) m -> p k m", p=P))
             by_cos = looked_up_product(f"by_cos{k}", cosines, values[:], 0, entries)
             by_sin = looked_up_product(f"by_sin{k}", sines, turned[:], 0, entries)
-            rotated = rounded_sum(f"rotated{k}", by_cos[:], by_sin[:])
+            rotated.append([rounded_sum(f"rotated{k}_{q}", by_cos[:, cols[q]], by_sin[:, cols[q]])
+                            for q in range(pieces)])
+        for k in range(last):
             for q in range(pieces):
-                accumulate(k, q, rotated[:, q * PIECE:(q + 1) * PIECE])
+                accumulate(k, q, rotated[k][q][:], slice(0, PIECE), closes=False)
 
         block = slice(last * P, rows)
-        cols = [slice(q * PIECE, (q + 1) * PIECE) for q in range(pieces)]
         cosines = load("cosines_last", tab[0, block, :])
         values = [load(f"values_last{q}", x0[block, cols[q]]) for q in range(EARLY)]
         turned = [load("turned_last0", x1[block, cols[0]])]
         sines = load("sines_last", tab[1, block, :])
+        nc.sync.dma_start(weights[:, last, :], w_rows[:, last, :])
         for q in range(1, pieces):
             if q >= EARLY:
                 values.append(load(f"values_last{q}", x0[block, cols[q]]))
@@ -80,12 +86,26 @@ def tile_lookup_rope_mul_none_kernel(tc, tab, x0, x1, w, offs, out):
 
         by_cos = [looked_up_product(f"by_cos_last{q}", cosines, values[q][:], q * PIECE, PIECE)
                   for q in range(EARLY)]
-        for q in range(pieces):
-            if q >= EARLY:
-                by_cos.append(looked_up_product(f"by_cos_last{q}", cosines, values[q][:], q * PIECE, PIECE))
-            by_sin = looked_up_product(f"by_sin_last{q}", sines, turned[q][:], q * PIECE, PIECE)
-            rotated = rounded_sum(f"rotated_last{q}", by_cos[q][:], by_sin[:])
-            accumulate(last, q, rotated[:])
+        steps = entries // STEP
+        per_piece = PIECE // STEP
+        by_sin = []
+        for s in range(steps + 1):
+            if s < steps:
+                q, part = divmod(s, per_piece)
+                if part == 0 and q >= EARLY:
+                    by_cos.append(looked_up_product(f"by_cos_last{q}", cosines, values[q][:],
+                                                    q * PIECE, PIECE))
+                by_sin.append(looked_up_product(f"by_sin_last{s}", sines,
+                                                turned[q][:, part * STEP:(part + 1) * STEP],
+                                                s * STEP, STEP))
+            if s == 0:
+                continue
+            q, part = divmod(s - 1, per_piece)
+            inside = slice(part * STEP, (part + 1) * STEP)
+            rotated_last = rounded_sum(f"rotated_last{s - 1}", by_cos[q][:, inside], by_sin[s - 1][:])
+            accumulate(last, q, rotated_last[:], inside, closes=(part == per_piece - 1))
+            if part < per_piece - 1:
+                continue
             for b, bank in enumerate(banks[q]):
                 staged = held.tile([P, per_bank, PIECE], F32, name=f"staged{q}_{b}")
                 if q == pieces - 1 and b == len(banks[q]) - 1:

@@ -8,7 +8,7 @@ BANK = 512
 GROUP = 16
 PIECE = 256
 STEP = 128
-EARLY = 2
+EARLY = 3
 
 FLOPS = 2 * 512 * 512 * 1024
 
@@ -25,6 +25,7 @@ def tile_lookup_rope_mul_none_kernel(tc, tab, x0, x1, w, offs, out):
 
     with (
         tc.tile_pool(name="held", bufs=1) as held,
+        tc.tile_pool(name="sin_ring", bufs=2) as sin_ring,
         tc.psum_pool(name="psum", bufs=1) as psum,
     ):
         def load(name, source):
@@ -32,8 +33,8 @@ def tile_lookup_rope_mul_none_kernel(tc, tab, x0, x1, w, offs, out):
             nc.sync.dma_start(tile[:], source)
             return tile
 
-        def looked_up_product(name, window, factor, first, count):
-            product = held.tile([P, count], F32, name=name)
+        def looked_up_product(name, window, factor, first, count, pool=held):
+            product = pool.tile([P, count], F32, name=name)
             entries_used = offsets[:, first // GROUP:(first + count) // GROUP]
             nc.vector.tensor_tensor(product[:], window[:].indirect(entries_used), factor, MULT)
             return product
@@ -62,9 +63,11 @@ def tile_lookup_rope_mul_none_kernel(tc, tab, x0, x1, w, offs, out):
             cosines = load(f"cosines{k}", tab[0, block, :])
             values = load(f"values{k}", x0[block, :])
             if k == last - 1:
-                nc.sync.dma_start(weights[:, :last, :], w_rows[:, :last, :])
+                nc.sync.dma_start(weights[:, :k, :], w_rows[:, :k, :])
             sines = load(f"sines{k}", tab[1, block, :])
             turned = load(f"turned{k}", x1[block, :])
+            if k == last - 1:
+                nc.sync.dma_start(weights[:, k, :], w_rows[:, k, :])
             by_cos = looked_up_product(f"by_cos{k}", cosines, values[:], 0, entries)
             by_sin = looked_up_product(f"by_sin{k}", sines, turned[:], 0, entries)
             rotated.append([rounded_sum(f"rotated{k}_{q}", by_cos[:, cols[q]], by_sin[:, cols[q]])
@@ -75,37 +78,27 @@ def tile_lookup_rope_mul_none_kernel(tc, tab, x0, x1, w, offs, out):
 
         block = slice(last * P, rows)
         cosines = load("cosines_last", tab[0, block, :])
-        values = [load(f"values_last{q}", x0[block, cols[q]]) for q in range(EARLY)]
+        values_early = load("values_early", x0[block, :EARLY * PIECE])
+        values = [values_early[:, cols[q]] for q in range(EARLY)]
         turned = [load("turned_last0", x1[block, cols[0]])]
         sines = load("sines_last", tab[1, block, :])
         nc.sync.dma_start(weights[:, last, :], w_rows[:, last, :])
         for q in range(1, pieces):
             if q >= EARLY:
-                values.append(load(f"values_last{q}", x0[block, cols[q]]))
+                values.append(load(f"values_last{q}", x0[block, cols[q]])[:])
             turned.append(load(f"turned_last{q}", x1[block, cols[q]]))
 
-        by_cos = [looked_up_product(f"by_cos_last{q}", cosines, values[q][:], q * PIECE, PIECE)
+        by_cos = [looked_up_product(f"by_cos_last{q}", cosines, values[q], q * PIECE, PIECE)
                   for q in range(EARLY)]
-        steps = entries // STEP
-        per_piece = PIECE // STEP
-        by_sin = []
-        for s in range(steps + 1):
-            if s < steps:
-                q, part = divmod(s, per_piece)
-                if part == 0 and q >= EARLY:
-                    by_cos.append(looked_up_product(f"by_cos_last{q}", cosines, values[q][:],
-                                                    q * PIECE, PIECE))
-                by_sin.append(looked_up_product(f"by_sin_last{s}", sines,
-                                                turned[q][:, part * STEP:(part + 1) * STEP],
-                                                s * STEP, STEP))
-            if s == 0:
-                continue
-            q, part = divmod(s - 1, per_piece)
-            inside = slice(part * STEP, (part + 1) * STEP)
-            rotated_last = rounded_sum(f"rotated_last{s - 1}", by_cos[q][:, inside], by_sin[s - 1][:])
-            accumulate(last, q, rotated_last[:], inside, closes=(part == per_piece - 1))
-            if part < per_piece - 1:
-                continue
+        parts = [slice(i * STEP, (i + 1) * STEP) for i in range(PIECE // STEP)]
+        for q in range(pieces):
+            if q >= EARLY:
+                by_cos.append(looked_up_product(f"by_cos_last{q}", cosines, values[q], q * PIECE, PIECE))
+            by_sin = [looked_up_product("by_sin_last", sines, turned[q][:, part],
+                                        q * PIECE + part.start, STEP, sin_ring) for part in parts]
+            for i, part in enumerate(parts):
+                rotated_last = rounded_sum(f"rotated_last{q}_{i}", by_cos[q][:, part], by_sin[i][:])
+                accumulate(last, q, rotated_last[:], part, closes=(i == len(parts) - 1))
             for b, bank in enumerate(banks[q]):
                 staged = held.tile([P, per_bank, PIECE], F32, name=f"staged{q}_{b}")
                 if q == pieces - 1 and b == len(banks[q]) - 1:

import concourse.mybir as mybir

F32, BF16, U16 = mybir.dt.float32, mybir.dt.bfloat16, mybir.dt.uint16
MULT, ADD = mybir.AluOpType.mult, mybir.AluOpType.add

P = 128
BANK = 512
GROUP = 16
PIECE = 256
STEP = 128
EARLY = 3

FLOPS = 2 * 512 * 512 * 1024


def tile_lookup_rope_mul_none_kernel(tc, tab, x0, x1, w, offs, out):
    nc = tc.nc
    rows, positions = tab.shape[1], tab.shape[2]
    entries, features = x0.shape[1], w.shape[1]
    row_blocks, out_blocks, pieces = rows // P, features // P, entries // PIECE
    per_bank = BANK // PIECE
    last = row_blocks - 1
    w_rows = w.rearrange("(k p) m -> p k m", p=P)
    out_rows = out.rearrange("(m p) j -> p m j", p=P)

    with (
        tc.tile_pool(name="held", bufs=1) as held,
        tc.tile_pool(name="sin_ring", bufs=2) as sin_ring,
        tc.psum_pool(name="psum", bufs=1) as psum,
    ):
        def load(name, source):
            tile = held.tile([P, source.shape[1]], F32, name=name)
            nc.sync.dma_start(tile[:], source)
            return tile

        def looked_up_product(name, window, factor, first, count, pool=held):
            product = pool.tile([P, count], F32, name=name)
            entries_used = offsets[:, first // GROUP:(first + count) // GROUP]
            nc.vector.tensor_tensor(product[:], window[:].indirect(entries_used), factor, MULT)
            return product

        def rounded_sum(name, by_cos, by_sin):
            rotated = held.tile([P, by_cos.shape[1]], BF16, name=name)
            nc.vector.tensor_tensor(rotated[:], by_cos, by_sin, ADD)
            return rotated

        def accumulate(k, q, rotated, inside, closes):
            for m in range(out_blocks):
                b, i = divmod(m, per_bank)
                nc.tensor.matmul(banks[q][b][:, i, inside], weights[:, k, m * P:(m + 1) * P], rotated,
                                 start=(k == 0 and i == 0), stop=(closes and i == per_bank - 1))

        offsets = held.tile([P, entries // GROUP], U16, name="offsets")
        nc.sync.dma_start(offsets[:], offs)
        weights = held.tile([P, row_blocks, features], BF16, name="weights")
        banks = [[psum.tile([P, per_bank, PIECE], F32, name=f"bank{q}_{b}")
                  for b in range(out_blocks // per_bank)] for q in range(pieces)]

        cols = [slice(q * PIECE, (q + 1) * PIECE) for q in range(pieces)]
        rotated = []
        for k in range(last):
            block = slice(k * P, (k + 1) * P)
            cosines = load(f"cosines{k}", tab[0, block, :])
            values = load(f"values{k}", x0[block, :])
            if k == last - 1:
                nc.sync.dma_start(weights[:, :k, :], w_rows[:, :k, :])
            sines = load(f"sines{k}", tab[1, block, :])
            turned = load(f"turned{k}", x1[block, :])
            if k == last - 1:
                nc.sync.dma_start(weights[:, k, :], w_rows[:, k, :])
            by_cos = looked_up_product(f"by_cos{k}", cosines, values[:], 0, entries)
            by_sin = looked_up_product(f"by_sin{k}", sines, turned[:], 0, entries)
            rotated.append([rounded_sum(f"rotated{k}_{q}", by_cos[:, cols[q]], by_sin[:, cols[q]])
                            for q in range(pieces)])
        for k in range(last):
            for q in range(pieces):
                accumulate(k, q, rotated[k][q][:], slice(0, PIECE), closes=False)

        block = slice(last * P, rows)
        cosines = load("cosines_last", tab[0, block, :])
        values_early = load("values_early", x0[block, :EARLY * PIECE])
        values = [values_early[:, cols[q]] for q in range(EARLY)]
        turned = [load("turned_last0", x1[block, cols[0]])]
        sines = load("sines_last", tab[1, block, :])
        nc.sync.dma_start(weights[:, last, :], w_rows[:, last, :])
        for q in range(1, pieces):
            if q >= EARLY:
                values.append(load(f"values_last{q}", x0[block, cols[q]])[:])
            turned.append(load(f"turned_last{q}", x1[block, cols[q]]))

        by_cos = [looked_up_product(f"by_cos_last{q}", cosines, values[q], q * PIECE, PIECE)
                  for q in range(EARLY)]
        parts = [slice(i * STEP, (i + 1) * STEP) for i in range(PIECE // STEP)]
        for q in range(pieces):
            if q >= EARLY:
                by_cos.append(looked_up_product(f"by_cos_last{q}", cosines, values[q], q * PIECE, PIECE))
            by_sin = [looked_up_product("by_sin_last", sines, turned[q][:, part],
                                        q * PIECE + part.start, STEP, sin_ring) for part in parts]
            for i, part in enumerate(parts):
                rotated_last = rounded_sum(f"rotated_last{q}_{i}", by_cos[q][:, part], by_sin[i][:])
                accumulate(last, q, rotated_last[:], part, closes=(i == len(parts) - 1))
            for b, bank in enumerate(banks[q]):
                staged = held.tile([P, per_bank, PIECE], F32, name=f"staged{q}_{b}")
                if q == pieces - 1 and b == len(banks[q]) - 1:
                    nc.vector.tensor_copy(staged[:], bank[:])
                else:
                    nc.scalar.copy(staged[:], bank[:])
                nc.sync.dma_start(out_rows[:, b * per_bank:(b + 1) * per_bank, cols[q]], staged[:])
